import numpy as np
import ml_dtypes

BF16 = ml_dtypes.bfloat16


def bf(x):
    return np.asarray(x, np.float32).astype(BF16)


def f32(x):
    return np.asarray(x, np.float32)


def f64(x):
    return np.asarray(x).astype(np.float64)


def striped(idx):
    return np.tile(idx.reshape(-1, 16).T, (8, 1))


S, K, M, N, D, V = 256, 256, 512, 128, 4, 32


def sigmoid(v):
    return 1.0 / (1.0 + np.exp(-v))


def setup_inputs():
    return {"table": bf(np.random.standard_normal((K, S))), "w": bf(np.random.standard_normal((K, M)) / np.sqrt(K)), "b": f32(0.5 * np.random.standard_normal((M, 1))), "offs": striped(np.random.permutation(S)[:N])}


def reference(table, w, b, offs):
    idx = offs[:16].T.reshape(-1)
    x = f64(table)[:, idx]
    y = f64(w).T @ x
    z = (y + f64(b)) * sigmoid(y + f64(b))
    return z.reshape(M, V, D).max(axis=2)

@@ -1,0 +1,61 @@
+import concourse.mybir as mybir
+
+BF16, F32, U16 = mybir.dt.bfloat16, mybir.dt.float32, mybir.dt.uint16
+SILU = mybir.ActivationFunctionType.Silu
+
+P = 128
+K, S = 256, 256
+M = 512
+N = 128
+NEIGHBOURS = 4
+NODES = N // NEIGHBOURS
+K_BLOCKS = K // P
+M_BLOCKS = M // P
+
+FLOPS = 2 * K * M * N
+
+
+def tile_gather_matmul_kernel(tc, table, w, b, offs, out):
+    nc = tc.nc
+    with (
+        tc.tile_pool(name="held", bufs=1) as held,
+        tc.psum_pool(name="banks", bufs=1) as banks,
+    ):
+        offsets = held.tile([P, N // 16], U16, name="offsets")
+        nc.sync.dma_start(offsets[:], offs)
+
+        table_blocks = []
+        weight_blocks = []
+        for k in range(K_BLOCKS):
+            table_block = held.tile([P, S], BF16, name=f"table{k}")
+            nc.sync.dma_start(table_block[:], table[k * P : (k + 1) * P, :])
+            table_blocks.append(table_block)
+            weight_block = held.tile([P, M], BF16, name=f"weights{k}")
+            nc.scalar.dma_start(weight_block[:], w[k * P : (k + 1) * P, :])
+            weight_blocks.append(weight_block)
+
+        bias = held.tile([P, M_BLOCKS], F32, name="bias")
+        with nc.allow_non_contiguous_dma(reason="one float32 to a partition for each block of features"):
+            nc.sync.dma_start(bias[:], b.rearrange("(a p) o -> p (a o)", p=P))
+
+        pooled = held.tile([P, M_BLOCKS, NODES], F32, name="pooled")
+        for a in range(M_BLOCKS):
+            bank = banks.tile([P, N], F32, name=f"bank{a}")
+            for k in range(K_BLOCKS):
+                nc.tensor.matmul(
+                    bank[:],
+                    weight_blocks[k][:, a * P : (a + 1) * P],
+                    table_blocks[k][:].indirect(offsets[:]),
+                    start=(k == 0),
+                    stop=(k == K_BLOCKS - 1),
+                )
+            activated = held.tile([P, N], F32, name=f"activated{a}")
+            nc.scalar.activation(activated[:], bank[:], SILU, bias=bias[:, a : a + 1])
+            nc.vector.tensor_reduce(
+                pooled[:, a, :],
+                activated[:].rearrange("p (v t) -> p v t", t=NEIGHBOURS),
+                axis=mybir.AxisListType.X,
+                op=mybir.AluOpType.max,
+            )
+
+        nc.sync.dma_start(out.rearrange("(a p) v -> p a v", p=P), pooled[:])

@@ -38,6 +38,10 @@ def tile_gather_matmul_kernel(tc, table, w, b, offs, out):
         with nc.allow_non_contiguous_dma(reason="one float32 to a partition for each block of features"):
             nc.sync.dma_start(bias[:], b.rearrange("(a p) o -> p (a o)", p=P))
 
+        scratch = held.tile([P, 1], F32, name="scratch")
+        nc.vector.memset(scratch[:], 0.0)
+        nc.scalar.activation(scratch[:], scratch[:], SILU)
+
         pooled = held.tile([P, M_BLOCKS, NODES], F32, name="pooled")
         for a in range(M_BLOCKS):
             bank = banks.tile([P, N], F32, name=f"bank{a}")

@@ -11,6 +11,8 @@ NEIGHBOURS = 4
 NODES = N // NEIGHBOURS
 K_BLOCKS = K // P
 M_BLOCKS = M // P
+SQUARE = 32
+SQUARES = P // SQUARE
 
 FLOPS = 2 * K * M * N
 
@@ -34,13 +36,18 @@ def tile_gather_matmul_kernel(tc, table, w, b, offs, out):
             nc.scalar.dma_start(weight_block[:], w[k * P : (k + 1) * P, :])
             weight_blocks.append(weight_block)
 
-        bias = held.tile([P, M_BLOCKS], F32, name="bias")
-        with nc.allow_non_contiguous_dma(reason="one float32 to a partition for each block of features"):
-            nc.sync.dma_start(bias[:], b.rearrange("(a p) o -> p (a o)", p=P))
-
         scratch = held.tile([P, 1], F32, name="scratch")
         nc.vector.memset(scratch[:], 0.0)
         nc.scalar.activation(scratch[:], scratch[:], SILU)
+
+        bias_rows = held.tile([P, M_BLOCKS * SQUARE], F32, name="bias_rows", align_bytes=64)
+        nc.vector.memset(bias_rows[:], 0.0)
+        nc.sync.dma_start(
+            bias_rows[0:P:SQUARE, :].rearrange("g (a i) -> g a i", i=SQUARE),
+            b.rearrange("(a g i) o -> g a (i o)", g=SQUARES, i=SQUARE),
+        )
+        bias_columns = held.tile([P, M_BLOCKS * SQUARE], F32, name="bias_columns", align_bytes=64)
+        nc.vector.transpose(bias_columns[:], bias_rows[:])
 
         pooled = held.tile([P, M_BLOCKS, NODES], F32, name="pooled")
         for a in range(M_BLOCKS):
@@ -54,7 +61,7 @@ def tile_gather_matmul_kernel(tc, table, w, b, offs, out):
                     stop=(k == K_BLOCKS - 1),
                 )
             activated = held.tile([P, N], F32, name=f"activated{a}")
-            nc.scalar.activation(activated[:], bank[:], SILU, bias=bias[:, a : a + 1])
+            nc.scalar.activation(activated[:], bank[:], SILU, bias=bias_columns[:, a * SQUARE : a * SQUARE + 1])
             nc.vector.tensor_reduce(
                 pooled[:, a, :],
                 activated[:].rearrange("p (v t) -> p v t", t=NEIGHBOURS),

@@ -23,22 +23,18 @@ def tile_gather_matmul_kernel(tc, table, w, b, offs, out):
         tc.tile_pool(name="held", bufs=1) as held,
         tc.psum_pool(name="banks", bufs=1) as banks,
     ):
-        offsets = held.tile([P, N // 16], U16, name="offsets")
-        nc.sync.dma_start(offsets[:], offs)
-
-        table_blocks = []
-        weight_blocks = []
-        for k in range(K_BLOCKS):
-            table_block = held.tile([P, S], BF16, name=f"table{k}")
-            nc.sync.dma_start(table_block[:], table[k * P : (k + 1) * P, :])
-            table_blocks.append(table_block)
-            weight_block = held.tile([P, M], BF16, name=f"weights{k}")
-            nc.scalar.dma_start(weight_block[:], w[k * P : (k + 1) * P, :])
-            weight_blocks.append(weight_block)
-
         scratch = held.tile([P, 1], F32, name="scratch")
         nc.vector.memset(scratch[:], 0.0)
         nc.scalar.activation(scratch[:], scratch[:], SILU)
+
+        offsets = held.tile([P, N // 16], U16, name="offsets")
+        nc.sync.dma_start(offsets[:], offs)
+
+        table_blocks = [held.tile([P, S], BF16, name=f"table{k}") for k in range(K_BLOCKS)]
+        weight_blocks = [held.tile([P, M], BF16, name=f"weights{k}") for k in range(K_BLOCKS)]
+        for k in range(K_BLOCKS):
+            nc.scalar.dma_start(weight_blocks[k][:], w[k * P : (k + 1) * P, :])
+        nc.sync.dma_start(table_blocks[0][:], table[0:P, :])
 
         bias_rows = held.tile([P, M_BLOCKS * SQUARE], F32, name="bias_rows", align_bytes=64)
         nc.vector.memset(bias_rows[:], 0.0)
@@ -48,6 +44,8 @@ def tile_gather_matmul_kernel(tc, table, w, b, offs, out):
         )
         bias_columns = held.tile([P, M_BLOCKS * SQUARE], F32, name="bias_columns", align_bytes=64)
         nc.vector.transpose(bias_columns[:], bias_rows[:])
+
+        nc.sync.dma_start(table_blocks[1][:], table[P : 2 * P, :])
 
         pooled = held.tile([P, M_BLOCKS, NODES], F32, name="pooled")
         for a in range(M_BLOCKS):

@@ -32,8 +32,8 @@ def tile_gather_matmul_kernel(tc, table, w, b, offs, out):
 
         table_blocks = [held.tile([P, S], BF16, name=f"table{k}") for k in range(K_BLOCKS)]
         weight_blocks = [held.tile([P, M], BF16, name=f"weights{k}") for k in range(K_BLOCKS)]
-        for k in range(K_BLOCKS):
-            nc.scalar.dma_start(weight_blocks[k][:], w[k * P : (k + 1) * P, :])
+        nc.scalar.dma_start(weight_blocks[0][:], w[0:P, :])
+        nc.scalar.dma_start(table_blocks[1][:], table[P : 2 * P, :])
         nc.sync.dma_start(table_blocks[0][:], table[0:P, :])
 
         bias_rows = held.tile([P, M_BLOCKS * SQUARE], F32, name="bias_rows", align_bytes=64)
@@ -45,7 +45,7 @@ def tile_gather_matmul_kernel(tc, table, w, b, offs, out):
         bias_columns = held.tile([P, M_BLOCKS * SQUARE], F32, name="bias_columns", align_bytes=64)
         nc.vector.transpose(bias_columns[:], bias_rows[:])
 
-        nc.sync.dma_start(table_blocks[1][:], table[P : 2 * P, :])
+        nc.sync.dma_start(weight_blocks[1][:], w[P : 2 * P, :])
 
         pooled = held.tile([P, M_BLOCKS, NODES], F32, name="pooled")
         for a in range(M_BLOCKS):

import concourse.mybir as mybir

BF16, F32, U16 = mybir.dt.bfloat16, mybir.dt.float32, mybir.dt.uint16
SILU = mybir.ActivationFunctionType.Silu

P = 128
K, S = 256, 256
M = 512
N = 128
NEIGHBOURS = 4
NODES = N // NEIGHBOURS
K_BLOCKS = K // P
M_BLOCKS = M // P
SQUARE = 32
SQUARES = P // SQUARE

FLOPS = 2 * K * M * N


def tile_gather_matmul_kernel(tc, table, w, b, offs, out):
    nc = tc.nc
    with (
        tc.tile_pool(name="held", bufs=1) as held,
        tc.psum_pool(name="banks", bufs=1) as banks,
    ):
        scratch = held.tile([P, 1], F32, name="scratch")
        nc.vector.memset(scratch[:], 0.0)
        nc.scalar.activation(scratch[:], scratch[:], SILU)

        offsets = held.tile([P, N // 16], U16, name="offsets")
        nc.sync.dma_start(offsets[:], offs)

        table_blocks = [held.tile([P, S], BF16, name=f"table{k}") for k in range(K_BLOCKS)]
        weight_blocks = [held.tile([P, M], BF16, name=f"weights{k}") for k in range(K_BLOCKS)]
        nc.scalar.dma_start(weight_blocks[0][:], w[0:P, :])
        nc.scalar.dma_start(table_blocks[1][:], table[P : 2 * P, :])
        nc.sync.dma_start(table_blocks[0][:], table[0:P, :])

        bias_rows = held.tile([P, M_BLOCKS * SQUARE], F32, name="bias_rows", align_bytes=64)
        nc.vector.memset(bias_rows[:], 0.0)
        nc.sync.dma_start(
            bias_rows[0:P:SQUARE, :].rearrange("g (a i) -> g a i", i=SQUARE),
            b.rearrange("(a g i) o -> g a (i o)", g=SQUARES, i=SQUARE),
        )
        bias_columns = held.tile([P, M_BLOCKS * SQUARE], F32, name="bias_columns", align_bytes=64)
        nc.vector.transpose(bias_columns[:], bias_rows[:])

        nc.sync.dma_start(weight_blocks[1][:], w[P : 2 * P, :])

        pooled = held.tile([P, M_BLOCKS, NODES], F32, name="pooled")
        for a in range(M_BLOCKS):
            bank = banks.tile([P, N], F32, name=f"bank{a}")
            for k in range(K_BLOCKS):
                nc.tensor.matmul(
                    bank[:],
                    weight_blocks[k][:, a * P : (a + 1) * P],
                    table_blocks[k][:].indirect(offsets[:]),
                    start=(k == 0),
                    stop=(k == K_BLOCKS - 1),
                )
            activated = held.tile([P, N], F32, name=f"activated{a}")
            nc.scalar.activation(activated[:], bank[:], SILU, bias=bias_columns[:, a * SQUARE : a * SQUARE + 1])
            nc.vector.tensor_reduce(
                pooled[:, a, :],
                activated[:].rearrange("p (v t) -> p v t", t=NEIGHBOURS),
                axis=mybir.AxisListType.X,
                op=mybir.AluOpType.max,
            )

        nc.sync.dma_start(out.rearrange("(a p) v -> p a v", p=P), pooled[:])
